import numpy as np
import ml_dtypes


def mxq(x, axis, fmt="e4m3"):
    dtype, down = {"e4m3": (ml_dtypes.float8_e4m3fn, 7), "e5m2": (ml_dtypes.float8_e5m2, 14)}[fmt]
    v = np.moveaxis(np.asarray(x, np.float32).astype(ml_dtypes.bfloat16).astype(np.float64), axis, -1)
    blocks = v.reshape(v.shape[:-1] + (-1, 32))
    amax = np.abs(blocks).max(-1, keepdims=True)
    byte = np.maximum(np.where(amax > 0, np.frexp(amax)[1] - 1 + 127, 0) - down, 1)
    scale = np.exp2(byte - 127.0)
    codes = (blocks / scale).astype(np.float32).astype(dtype).astype(np.float64)
    return np.moveaxis((codes * scale).reshape(v.shape), -1, axis)


WIDE = False


def mx_kscale(k):
    if not WIDE:
        return np.ones(k)
    levels = np.array([10, -10, 5, -5, 0])
    if k % 512:
        return np.exp2(np.random.permutation(np.resize(levels, k // 32))).repeat(32)
    a = np.empty((k // 512, 16))
    for p in range(k // 512):
        a[p, :8] = np.random.permutation(np.resize(levels, 8))
        for g in range(8):
            far = levels[np.abs(levels - a[p, g]) >= 10]
            a[p, g + 8] = far[np.random.randint(len(far))]
    return np.exp2(a.ravel()).repeat(32)


def f64(x):
    return np.asarray(x).astype(np.float64)


def striped(idx):
    return np.tile(np.asarray(idx).reshape(-1, 16).T, (8, 1)).astype(np.uint16)


def unstriped(offs):
    return offs[:16].T.reshape(-1).astype(np.int64)


E2M1 = np.array([0.0, 0.5, 1.0, 1.5, 2.0, 3.0, 4.0, 6.0, -0.0, -0.5, -1.0, -1.5, -2.0, -3.0, -4.0, -6.0])


def pack_weight(w, fmt):
    k, n = w.shape
    w = f64(np.asarray(w, np.float32).astype(ml_dtypes.bfloat16)).reshape(k // 32, 32, n)
    amax = np.abs(w).max(1)
    if fmt == "e4m3":
        byte = np.frexp(amax)[1] - 1 + 127 - 7
    else:
        mant, ex = np.frexp(amax / 6.0)
        byte = np.where(mant > 0.5, ex, ex - 1) + 127
    byte = np.clip(np.where(amax > 0, byte, 1), 1, 254)
    scaled = (w * np.exp2(127.0 - byte)[:, None, :]).reshape(k, n).astype(np.float32)
    by_word = np.ascontiguousarray(scaled.reshape(k // 512, 128, 4, n).transpose(0, 1, 3, 2))
    if fmt == "e4m3":
        words = by_word.astype(ml_dtypes.float8_e4m3fn).view(np.uint8)
    else:
        c = by_word.astype(ml_dtypes.float4_e2m1fn).view(np.uint8) & 0xF
        words = (c[..., 0::2] | (c[..., 1::2] << 4)).reshape(k // 512, 128, 2 * n)
    return np.ascontiguousarray(words), np.ascontiguousarray(byte.astype(np.uint8).reshape(k // 512, 16, n))


def unpack_weight(words, scales, fmt):
    g, _, n = scales.shape
    words = np.ascontiguousarray(words).reshape(g, 128, n, -1)
    if fmt == "e4m3":
        vals = words.view(ml_dtypes.float8_e4m3fn).astype(np.float64)
    else:
        nib = np.empty((g, 128, n, 4), np.uint8)
        nib[..., 0::2] = words & 0xF
        nib[..., 1::2] = words >> 4
        vals = E2M1[nib]
    vals = vals * np.repeat(np.exp2(scales.astype(np.float64) - 127.0), 8, axis=1)[..., None]
    return vals.transpose(0, 1, 3, 2).reshape(g * 512, n)


def softplus(v):
    return np.log(1.0 + np.exp(v))


def sigmoid(v):
    return 1.0 / (1.0 + np.exp(-v))


D, E, T, I, Q = 512, 512, 2048, 512, 128


def setup_inputs():
    n = np.random.standard_normal
    idx = np.random.permutation(T)[:I]
    fd = mx_kscale(D)
    fe = mx_kscale(E)
    keysp = pack_weight(n((D, T)) / fd[:, None], "e4m3")
    valsp = pack_weight(n((E, T)) / fe[:, None], "e4m3")
    return {
        "query": (n((D, Q)) * 0.6 / np.sqrt(D) * fd[:, None]).astype(np.float32),
        "query2": (n((D, Q)) * 1.0 / np.sqrt(D) * fd[:, None]).astype(np.float32),
        "keys_words": keysp[0],
        "keys_scales": keysp[1],
        "strict": (np.random.uniform(0.4, 1.2, (Q, 1))).astype(np.float32),
        "gout": (n((E, Q)) * 1 / np.sqrt(E) * fe[:, None]).astype(np.float32),
        "vals_words": valsp[0],
        "vals_scales": valsp[1],
        "old": (0.5 * n((Q, T))).astype(np.float32),
        "offs": striped(idx),
    }


def reference(query, query2, keys_words, keys_scales, strict, gout, vals_words, vals_scales, old, offs):
    idx = unstriped(offs)
    keysu = unpack_weight(keys_words, keys_scales, "e4m3")
    valsu = unpack_weight(vals_words, vals_scales, "e4m3")
    queryq = mxq(f64(query), 0, "e4m3")
    keysidxg = keysu[:, idx]
    a = queryq.T @ keysidxg
    query2q = mxq(f64(query2), 0, "e4m3")
    b = query2q.T @ keysidxg
    s = a - softplus(b) * f64(strict)
    p = np.exp(s - np.max(s, axis=1, keepdims=True))
    z = np.sum(p, axis=1, keepdims=True)
    goutq = mxq(f64(gout), 0, "e4m3")
    valsidxg = valsu[:, idx]
    c0 = goutq.T @ valsidxg
    dz = np.sum(c0 * p / np.square(z) * (-1.0), axis=1, keepdims=True)
    dp = c0 / z + dz
    ds = dp * p
    db = ds * (-1.0) * f64(strict) * sigmoid(b)
    gs = db * 512.0
    gf = np.zeros((Q, T))
    gf[:, idx] = gs
    y = f64(old) + gf
    return y

@@ -1,0 +1,165 @@
+from contextlib import ExitStack
+
+import concourse.mybir as mybir
+
+F32 = mybir.dt.float32
+BF16 = mybir.dt.bfloat16
+I32 = mybir.dt.int32
+U32 = mybir.dt.uint32
+U16 = mybir.dt.uint16
+U8 = mybir.dt.uint8
+FP8X4 = mybir.dt.float8_e4m3fn_x4
+ALU = mybir.AluOpType
+ACT = mybir.ActivationFunctionType
+AXIS_X = mybir.AxisListType.X
+
+P = 128
+PACK = 4
+T = 2048
+SLOTS = 512
+HALF = SLOTS // 2
+Q = 128
+GAIN = 512.0
+LN_FLOOR = 2.0 ** -60
+OUT_WIDTHS = (512, 640, 576, 320)
+
+FLOPS = 3 * 2 * 512 * Q * SLOTS
+
+
+def tile_attend_bheldback_s_kernel(tc, query, query2, keys_words, keys_scales, strict, gout,
+                                    vals_words, vals_scales, old, offs, out):
+    nc = tc.nc
+    with ExitStack() as ctx:
+        sb = ctx.enter_context(tc.tile_pool(name="sb", bufs=1))
+        ps = ctx.enter_context(tc.psum_pool(name="ps", bufs=1))
+
+        offsets = sb.tile([P, SLOTS // 16], U16, name="offsets")
+        nc.sync.dma_start(offsets[:], offs)
+
+        def by_word(x):
+            return x.rearrange("(p j) w -> p j w", j=PACK)
+
+        def load_words(tile, words):
+            nc.sync.dma_start(tile[:].bitcast(I32), words[0].rearrange("p n t -> p (n t)").bitcast(I32))
+
+        def load_scale_rows(queue, tile, scales):
+            for r in range(4):
+                queue.dma_start(tile[r:P:32, :].bitcast(I32), scales[0][r:16:4, :].bitcast(I32))
+
+        q2_raw = sb.tile([P, PACK, Q], F32, name="q2_raw", tag="slot_v")
+        nc.sync.dma_start(q2_raw[:], by_word(query2))
+        k_words = sb.tile([P, T], U32, name="k_words", tag="pool_a")
+        load_words(k_words, keys_words)
+        q_raw = sb.tile([P, PACK, Q], F32, name="q_raw")
+        nc.sync.dma_start(q_raw[:], by_word(query))
+
+        k_bytes = sb.tile([P, T], U8, name="k_bytes", tag="slot_kg", align_bytes=64)
+        v_bytes = sb.tile([P, T], U8, name="v_bytes", tag="slot_vg", align_bytes=64)
+        nc.vector.memset(k_bytes[:].bitcast(I32), 0)
+        load_scale_rows(nc.scalar, k_bytes, keys_scales)
+        nc.gpsimd.memset(v_bytes[:].bitcast(I32), 0)
+        load_scale_rows(nc.gpsimd, v_bytes, vals_scales)
+        strict_col = sb.tile([P, 1], F32, name="strict_col")
+        nc.gpsimd.dma_start(strict_col[:], strict)
+        warm_in = sb.tile([P, 1], F32, name="warm_in")
+        warm_out = sb.tile([P, 1], F32, name="warm_out")
+        nc.vector.memset(warm_in[:], 0.0)
+        nc.scalar.activation(warm_out[:], warm_in[:], ACT.Sigmoid)
+        placed = sb.tile([P, T], F32, name="placed")
+        nc.vector.memset(placed[:], 0.0)
+
+        q2_bf = sb.tile([P, Q, PACK], BF16, name="q2_bf", tag="slot_g", align_bytes=64)
+        nc.scalar.activation(q2_bf[:], q2_raw[:].rearrange("p j w -> p w j"), ACT.Copy)
+        kg_bytes = sb.tile([P, SLOTS], U8, name="kg_bytes", align_bytes=64)
+        nc.vector.tensor_copy(kg_bytes[:], k_bytes[:].indirect(offsets[:]))
+        q2_codes = sb.tile([P, Q], U32, name="q2_codes", align_bytes=64)
+        q2_scales = sb.tile([P, Q], U8, name="q2_scales", align_bytes=64)
+        nc.vector.quantize_mx(out=q2_codes[:].bitcast(FP8X4), scales=q2_scales[:],
+                              in_=q2_bf[:].rearrange("p w j -> p (w j)"))
+
+        v_words = sb.tile([P, T], U32, name="v_words", tag="slot_v")
+        load_words(v_words, vals_words)
+        g_raw = sb.tile([P, PACK, Q], F32, name="g_raw", tag="slot_g", align_bytes=64)
+        nc.sync.dma_start(g_raw[:], by_word(gout))
+
+        kg_words = sb.tile([P, SLOTS], U32, name="kg_words", tag="slot_kg", align_bytes=64)
+        halves = [slice(h * HALF, (h + 1) * HALF) for h in range(2)]
+        b_ps = [ps.tile([P, HALF], F32, name="b_ps%d" % h) for h in range(2)]
+        sig_neg = sb.tile([P, SLOTS], F32, name="sig_neg")
+        for h in range(2):
+            cols = halves[h]
+            nc.vector.tensor_copy(kg_words[:, cols],
+                                  k_words[:].indirect(offsets[:, h * HALF // 16:(h + 1) * HALF // 16]))
+            nc.tensor.matmul_mx(out=b_ps[h][:], lhsT=q2_codes[:].bitcast(FP8X4), lhsT_scale=q2_scales[:],
+                                rhs=kg_words[:, cols].bitcast(FP8X4), rhs_scale=kg_bytes[:, cols],
+                                start=True, stop=True)
+            nc.scalar.activation(sig_neg[:, cols], b_ps[h][:], ACT.Sigmoid, scale=-1.0)
+
+        old_sb = sb.tile([P, T], F32, name="old_sb", tag="pool_a")
+        nc.sync.dma_start(old_sb[:], old)
+
+        log_sig = sb.tile([P, SLOTS], F32, name="log_sig")
+        for h in range(2):
+            nc.scalar.activation(log_sig[:, halves[h]], sig_neg[:, halves[h]], ACT.Ln, bias=LN_FLOOR)
+
+        q_bf = sb.tile([P, Q, PACK], BF16, name="q_bf", align_bytes=64)
+        nc.vector.tensor_copy(q_bf[:], q_raw[:].rearrange("p j w -> p w j"))
+        vg_bytes = sb.tile([P, SLOTS], U8, name="vg_bytes", align_bytes=64)
+        nc.vector.tensor_copy(vg_bytes[:], v_bytes[:].indirect(offsets[:]))
+        q_codes = sb.tile([P, Q], U32, name="q_codes", align_bytes=64)
+        q_scales = sb.tile([P, Q], U8, name="q_scales", align_bytes=64)
+        nc.vector.quantize_mx(out=q_codes[:].bitcast(FP8X4), scales=q_scales[:],
+                              in_=q_bf[:].rearrange("p w j -> p (w j)"))
+        a_ps = ps.tile([P, SLOTS], F32, name="a_ps")
+        nc.tensor.matmul_mx(out=a_ps[:], lhsT=q_codes[:].bitcast(FP8X4), lhsT_scale=q_scales[:],
+                            rhs=kg_words[:].bitcast(FP8X4), rhs_scale=kg_bytes[:], start=True, stop=True)
+        vg_words = sb.tile([P, SLOTS], U32, name="vg_words", tag="slot_vg", align_bytes=64)
+        nc.vector.tensor_copy(vg_words[:], v_words[:].indirect(offsets[:]))
+        g_bf = sb.tile([P, Q, PACK], BF16, name="g_bf", align_bytes=64)
+        nc.vector.tensor_copy(g_bf[:], g_raw[:].rearrange("p j w -> p w j"))
+        gain_col = sb.tile([P, 1], F32, name="gain_col")
+        nc.vector.tensor_scalar(gain_col[:], strict_col[:], GAIN, None, ALU.mult)
+        g_codes = sb.tile([P, Q], U32, name="g_codes", align_bytes=64)
+        g_scales = sb.tile([P, Q], U8, name="g_scales", align_bytes=64)
+        nc.vector.quantize_mx(out=g_codes[:].bitcast(FP8X4), scales=g_scales[:],
+                              in_=g_bf[:].rearrange("p w j -> p (w j)"))
+        c_ps = ps.tile([P, SLOTS], F32, name="c_ps")
+        nc.tensor.matmul_mx(out=c_ps[:], lhsT=g_codes[:].bitcast(FP8X4), lhsT_scale=g_scales[:],
+                            rhs=vg_words[:].bitcast(FP8X4), rhs_scale=vg_bytes[:], start=True, stop=True)
+
+        neg_sp = sb.tile([P, SLOTS], F32, name="neg_sp", tag="slot_v")
+        s = sb.tile([P, SLOTS], F32, name="s")
+        for h in range(2):
+            nc.vector.scalar_tensor_tensor(neg_sp[:, halves[h]], b_ps[h][:], -1.0, log_sig[:, halves[h]],
+                                           ALU.mult, ALU.min)
+        for h in range(2):
+            nc.vector.scalar_tensor_tensor(s[:, halves[h]], neg_sp[:, halves[h]], strict_col[:],
+                                           a_ps[:, halves[h]], ALU.mult, ALU.add)
+        neg_max = sb.tile([P, 1], F32, name="neg_max")
+        nc.vector.tensor_reduce(neg_max[:], s[:], AXIS_X, ALU.max, negate=True)
+        gate = sb.tile([P, SLOTS], F32, name="gate")
+        nc.vector.tensor_scalar(gate[:], sig_neg[:], -1.0, gain_col[:], ALU.add, ALU.mult)
+
+        p = sb.tile([P, SLOTS], F32, name="p")
+        z = sb.tile([P, 1], F32, name="z")
+        nc.scalar.activation(p[:], s[:], ACT.Exp, bias=neg_max[:], accum_out=z[:])
+        z_inv = sb.tile([P, 1], F32, name="z_inv")
+        nc.vector.reciprocal(z_inv[:], z[:])
+        neg_cp = sb.tile([P, SLOTS], F32, name="neg_cp")
+        neg_sum = sb.tile([P, 1], F32, name="neg_sum")
+        nc.vector.scalar_tensor_tensor(neg_cp[:], c_ps[:], -1.0, p[:], ALU.mult, ALU.mult, accum_out=neg_sum[:])
+        z_inv2 = sb.tile([P, 1], F32, name="z_inv2")
+        nc.scalar.activation(z_inv2[:], z_inv[:], ACT.Square)
+        centred = sb.tile([P, SLOTS], F32, name="centred")
+        nc.scalar.activation(centred[:], c_ps[:], ACT.Identity, bias=neg_sum[:], scale=z[:])
+        weight = sb.tile([P, SLOTS], F32, name="weight")
+        nc.vector.scalar_tensor_tensor(weight[:], p[:], z_inv2[:], gate[:], ALU.mult, ALU.mult)
+        nc.vector.tensor_tensor(placed[:].indirect(offsets[:]), weight[:], centred[:], ALU.mult)
+
+        start = 0
+        for n, width in enumerate(OUT_WIDTHS):
+            cols = slice(start, start + width)
+            total = sb.tile([P, width], F32, name="total%d" % n)
+            nc.vector.tensor_tensor(total[:], placed[:, cols], old_sb[:, cols], ALU.add)
+            nc.sync.dma_start(out[:, cols], total[:])
+            start = start + width

@@ -21,7 +21,7 @@ HALF = SLOTS // 2
 Q = 128
 GAIN = 512.0
 LN_FLOOR = 2.0 ** -60
-OUT_WIDTHS = (512, 640, 576, 320)
+OUT_WIDTHS = (256, 512, 512, 512, 256)
 
 FLOPS = 3 * 2 * 512 * Q * SLOTS
 
@@ -33,133 +33,144 @@ def tile_attend_bheldback_s_kernel(tc, query, query2, keys_words, keys_scales, s
         sb = ctx.enter_context(tc.tile_pool(name="sb", bufs=1))
         ps = ctx.enter_context(tc.psum_pool(name="ps", bufs=1))
 
+        def tile(name, shape, dtype, slot=None):
+            return sb.tile(shape, dtype, name=name, tag=slot or name, align_bytes=64)
+
+        def load_rows(raw, x):
+            nc.sync.dma_start(raw[:], x.rearrange("(p j) w -> p j w", j=PACK))
+
+        def load_words(pool_words, words):
+            nc.sync.dma_start(pool_words[:].bitcast(I32), words[0].rearrange("p n t -> p (n t)").bitcast(I32))
+
+        def load_scale_rows(pool_bytes, scales):
+            for r in range(4):
+                nc.sync.dma_start(pool_bytes[r:P:32, :].bitcast(I32), scales[0][r:16:4, :].bitcast(I32))
+
+        def quantise(codes, scale_bytes, grouped):
+            nc.vector.quantize_mx(out=codes[:].bitcast(FP8X4), scales=scale_bytes[:],
+                                  in_=grouped[:].rearrange("p w j -> p (w j)"))
+
+        def product(acc, lhs_codes, lhs_scales, words, scale_bytes):
+            nc.tensor.matmul_mx(out=acc, lhsT=lhs_codes.bitcast(FP8X4), lhsT_scale=lhs_scales,
+                                rhs=words.bitcast(FP8X4), rhs_scale=scale_bytes, start=True, stop=True)
+
         offsets = sb.tile([P, SLOTS // 16], U16, name="offsets")
         nc.sync.dma_start(offsets[:], offs)
+        q2_raw = tile("q2_raw", [P, PACK, Q], F32, "slot_vw")
+        load_rows(q2_raw, query2)
 
-        def by_word(x):
-            return x.rearrange("(p j) w -> p j w", j=PACK)
-
-        def load_words(tile, words):
-            nc.sync.dma_start(tile[:].bitcast(I32), words[0].rearrange("p n t -> p (n t)").bitcast(I32))
-
-        def load_scale_rows(queue, tile, scales):
-            for r in range(4):
-                queue.dma_start(tile[r:P:32, :].bitcast(I32), scales[0][r:16:4, :].bitcast(I32))
-
-        q2_raw = sb.tile([P, PACK, Q], F32, name="q2_raw", tag="slot_v")
-        nc.sync.dma_start(q2_raw[:], by_word(query2))
-        k_words = sb.tile([P, T], U32, name="k_words", tag="pool_a")
-        load_words(k_words, keys_words)
-        q_raw = sb.tile([P, PACK, Q], F32, name="q_raw")
-        nc.sync.dma_start(q_raw[:], by_word(query))
-
-        k_bytes = sb.tile([P, T], U8, name="k_bytes", tag="slot_kg", align_bytes=64)
-        v_bytes = sb.tile([P, T], U8, name="v_bytes", tag="slot_vg", align_bytes=64)
-        nc.vector.memset(k_bytes[:].bitcast(I32), 0)
-        load_scale_rows(nc.scalar, k_bytes, keys_scales)
-        nc.gpsimd.memset(v_bytes[:].bitcast(I32), 0)
-        load_scale_rows(nc.gpsimd, v_bytes, vals_scales)
-        strict_col = sb.tile([P, 1], F32, name="strict_col")
-        nc.gpsimd.dma_start(strict_col[:], strict)
-        warm_in = sb.tile([P, 1], F32, name="warm_in")
-        warm_out = sb.tile([P, 1], F32, name="warm_out")
-        nc.vector.memset(warm_in[:], 0.0)
+        warm_in = tile("warm_in", [P, 1], F32, "slot_q")
+        warm_out = tile("warm_out", [P, 1], F32, "slot_vb")
+        nc.gpsimd.memset(warm_in[:], 0.0)
         nc.scalar.activation(warm_out[:], warm_in[:], ACT.Sigmoid)
-        placed = sb.tile([P, T], F32, name="placed")
+
+        one_col = tile("one_col", [P, 1], F32, "slot_kw")
+        nc.gpsimd.memset(one_col[:], 1.0)
+        k_bytes = tile("k_bytes", [P, T], U8, "slot_kb")
+        nc.vector.memset(k_bytes[:].bitcast(I32), 0)
+        load_scale_rows(k_bytes, keys_scales)
+        floor_col = tile("floor_col", [P, 1], F32)
+        nc.vector.tensor_scalar(floor_col[:], one_col[:], LN_FLOOR, None, ALU.mult)
+        k_words = tile("k_words", [P, T], U32, "slot_kw")
+        load_words(k_words, keys_words)
+        q_raw = tile("q_raw", [P, PACK, Q], F32, "slot_q")
+        load_rows(q_raw, query)
+        placed = tile("placed", [P, T], F32)
         nc.vector.memset(placed[:], 0.0)
+        v_bytes = tile("v_bytes", [P, T], U8, "slot_vb")
+        nc.vector.memset(v_bytes[:].bitcast(I32), 0)
+        load_scale_rows(v_bytes, vals_scales)
 
-        q2_bf = sb.tile([P, Q, PACK], BF16, name="q2_bf", tag="slot_g", align_bytes=64)
+        q2_bf = tile("q2_bf", [P, Q, PACK], BF16, "slot_g")
         nc.scalar.activation(q2_bf[:], q2_raw[:].rearrange("p j w -> p w j"), ACT.Copy)
-        kg_bytes = sb.tile([P, SLOTS], U8, name="kg_bytes", align_bytes=64)
-        nc.vector.tensor_copy(kg_bytes[:], k_bytes[:].indirect(offsets[:]))
-        q2_codes = sb.tile([P, Q], U32, name="q2_codes", align_bytes=64)
-        q2_scales = sb.tile([P, Q], U8, name="q2_scales", align_bytes=64)
-        nc.vector.quantize_mx(out=q2_codes[:].bitcast(FP8X4), scales=q2_scales[:],
-                              in_=q2_bf[:].rearrange("p w j -> p (w j)"))
-
-        v_words = sb.tile([P, T], U32, name="v_words", tag="slot_v")
+        v_words = tile("v_words", [P, T], U32, "slot_vw")
         load_words(v_words, vals_words)
-        g_raw = sb.tile([P, PACK, Q], F32, name="g_raw", tag="slot_g", align_bytes=64)
-        nc.sync.dma_start(g_raw[:], by_word(gout))
 
-        kg_words = sb.tile([P, SLOTS], U32, name="kg_words", tag="slot_kg", align_bytes=64)
+        kg_bytes = tile("kg_bytes", [P, SLOTS], U8)
+        nc.vector.tensor_copy(kg_bytes[:], k_bytes[:].indirect(offsets[:]))
+        q2_codes = tile("q2_codes", [P, Q], U32)
+        q2_scales = tile("q2_scales", [P, Q], U8)
+        quantise(q2_codes, q2_scales, q2_bf)
+        g_raw = tile("g_raw", [P, PACK, Q], F32, "slot_g")
+        load_rows(g_raw, gout)
+
+        q_bf = tile("q_bf", [P, Q, PACK], BF16)
+        nc.scalar.activation(q_bf[:], q_raw[:].rearrange("p j w -> p w j"), ACT.Copy)
+        strict_col = tile("strict_col", [P, 1], F32, "slot_q")
+        nc.sync.dma_start(strict_col[:], strict)
+
+        kg_words = tile("kg_words", [P, SLOTS], U32, "slot_kb")
         halves = [slice(h * HALF, (h + 1) * HALF) for h in range(2)]
         b_ps = [ps.tile([P, HALF], F32, name="b_ps%d" % h) for h in range(2)]
-        sig_neg = sb.tile([P, SLOTS], F32, name="sig_neg")
+        sig_neg = tile("sig_neg", [P, SLOTS], F32)
         for h in range(2):
             cols = halves[h]
             nc.vector.tensor_copy(kg_words[:, cols],
                                   k_words[:].indirect(offsets[:, h * HALF // 16:(h + 1) * HALF // 16]))
-            nc.tensor.matmul_mx(out=b_ps[h][:], lhsT=q2_codes[:].bitcast(FP8X4), lhsT_scale=q2_scales[:],
-                                rhs=kg_words[:, cols].bitcast(FP8X4), rhs_scale=kg_bytes[:, cols],
-                                start=True, stop=True)
+            product(b_ps[h][:], q2_codes[:], q2_scales[:], kg_words[:, cols], kg_bytes[:, cols])
             nc.scalar.activation(sig_neg[:, cols], b_ps[h][:], ACT.Sigmoid, scale=-1.0)
+        q_codes = tile("q_codes", [P, Q], U32)
+        q_scales = tile("q_scales", [P, Q], U8)
+        quantise(q_codes, q_scales, q_bf)
+        a_ps = ps.tile([P, SLOTS], F32, name="a_ps")
+        product(a_ps[:], q_codes[:], q_scales[:], kg_words[:], kg_bytes[:])
 
-        old_sb = sb.tile([P, T], F32, name="old_sb", tag="pool_a")
+        old_sb = tile("old_sb", [P, T], F32, "slot_kw")
         nc.sync.dma_start(old_sb[:], old)
 
-        log_sig = sb.tile([P, SLOTS], F32, name="log_sig")
+        log_sig = tile("log_sig", [P, SLOTS], F32)
         for h in range(2):
-            nc.scalar.activation(log_sig[:, halves[h]], sig_neg[:, halves[h]], ACT.Ln, bias=LN_FLOOR)
+            nc.scalar.activation(log_sig[:, halves[h]], sig_neg[:, halves[h]], ACT.Ln, bias=floor_col[:])
 
-        q_bf = sb.tile([P, Q, PACK], BF16, name="q_bf", align_bytes=64)
-        nc.vector.tensor_copy(q_bf[:], q_raw[:].rearrange("p j w -> p w j"))
-        vg_bytes = sb.tile([P, SLOTS], U8, name="vg_bytes", align_bytes=64)
+        vg_bytes = tile("vg_bytes", [P, SLOTS], U8)
         nc.vector.tensor_copy(vg_bytes[:], v_bytes[:].indirect(offsets[:]))
-        q_codes = sb.tile([P, Q], U32, name="q_codes", align_bytes=64)
-        q_scales = sb.tile([P, Q], U8, name="q_scales", align_bytes=64)
-        nc.vector.quantize_mx(out=q_codes[:].bitcast(FP8X4), scales=q_scales[:],
-                              in_=q_bf[:].rearrange("p w j -> p (w j)"))
-        a_ps = ps.tile([P, SLOTS], F32, name="a_ps")
-        nc.tensor.matmul_mx(out=a_ps[:], lhsT=q_codes[:].bitcast(FP8X4), lhsT_scale=q_scales[:],
-                            rhs=kg_words[:].bitcast(FP8X4), rhs_scale=kg_bytes[:], start=True, stop=True)
-        vg_words = sb.tile([P, SLOTS], U32, name="vg_words", tag="slot_vg", align_bytes=64)
+        vg_words = tile("vg_words", [P, SLOTS], U32, "slot_vb")
         nc.vector.tensor_copy(vg_words[:], v_words[:].indirect(offsets[:]))
-        g_bf = sb.tile([P, Q, PACK], BF16, name="g_bf", align_bytes=64)
-        nc.vector.tensor_copy(g_bf[:], g_raw[:].rearrange("p j w -> p w j"))
-        gain_col = sb.tile([P, 1], F32, name="gain_col")
-        nc.vector.tensor_scalar(gain_col[:], strict_col[:], GAIN, None, ALU.mult)
-        g_codes = sb.tile([P, Q], U32, name="g_codes", align_bytes=64)
-        g_scales = sb.tile([P, Q], U8, name="g_scales", align_bytes=64)
-        nc.vector.quantize_mx(out=g_codes[:].bitcast(FP8X4), scales=g_scales[:],
-                              in_=g_bf[:].rearrange("p w j -> p (w j)"))
-        c_ps = ps.tile([P, SLOTS], F32, name="c_ps")
-        nc.tensor.matmul_mx(out=c_ps[:], lhsT=g_codes[:].bitcast(FP8X4), lhsT_scale=g_scales[:],
-                            rhs=vg_words[:].bitcast(FP8X4), rhs_scale=vg_bytes[:], start=True, stop=True)
+        g_bf = tile("g_bf", [P, Q, PACK], BF16)
+        nc.gpsimd.tensor_scalar(g_bf[:], g_raw[:].rearrange("p j w -> p w j"), 1.0, 0.0, ALU.mult, ALU.add)
+        gain_col = tile("gain_col", [P, 1], F32)
+        nc.gpsimd.tensor_scalar(gain_col[:], strict_col[:], GAIN, 0.0, ALU.mult, ALU.add)
+        neg_gain_col = tile("neg_gain_col", [P, 1], F32)
+        nc.gpsimd.tensor_scalar(neg_gain_col[:], strict_col[:], -GAIN, 0.0, ALU.mult, ALU.add)
 
-        neg_sp = sb.tile([P, SLOTS], F32, name="neg_sp", tag="slot_v")
-        s = sb.tile([P, SLOTS], F32, name="s")
+        neg_sp = tile("neg_sp", [P, SLOTS], F32, "slot_vw")
+        s = tile("s", [P, SLOTS], F32, "slot_s")
         for h in range(2):
             nc.vector.scalar_tensor_tensor(neg_sp[:, halves[h]], b_ps[h][:], -1.0, log_sig[:, halves[h]],
                                            ALU.mult, ALU.min)
         for h in range(2):
             nc.vector.scalar_tensor_tensor(s[:, halves[h]], neg_sp[:, halves[h]], strict_col[:],
                                            a_ps[:, halves[h]], ALU.mult, ALU.add)
-        neg_max = sb.tile([P, 1], F32, name="neg_max")
+        g_codes = tile("g_codes", [P, Q], U32)
+        g_scales = tile("g_scales", [P, Q], U8)
+        quantise(g_codes, g_scales, g_bf)
+        c_ps = ps.tile([P, SLOTS], F32, name="c_ps")
+        product(c_ps[:], g_codes[:], g_scales[:], vg_words[:], vg_bytes[:])
+        neg_max = tile("neg_max", [P, 1], F32)
         nc.vector.tensor_reduce(neg_max[:], s[:], AXIS_X, ALU.max, negate=True)
-        gate = sb.tile([P, SLOTS], F32, name="gate")
-        nc.vector.tensor_scalar(gate[:], sig_neg[:], -1.0, gain_col[:], ALU.add, ALU.mult)
 
-        p = sb.tile([P, SLOTS], F32, name="p")
-        z = sb.tile([P, 1], F32, name="z")
+        p = tile("p", [P, SLOTS], F32)
+        z = tile("z", [P, 1], F32)
         nc.scalar.activation(p[:], s[:], ACT.Exp, bias=neg_max[:], accum_out=z[:])
-        z_inv = sb.tile([P, 1], F32, name="z_inv")
+        z_inv = tile("z_inv", [P, 1], F32)
         nc.vector.reciprocal(z_inv[:], z[:])
-        neg_cp = sb.tile([P, SLOTS], F32, name="neg_cp")
-        neg_sum = sb.tile([P, 1], F32, name="neg_sum")
+        neg_cp = tile("neg_cp", [P, SLOTS], F32)
+        neg_sum = tile("neg_sum", [P, 1], F32)
         nc.vector.scalar_tensor_tensor(neg_cp[:], c_ps[:], -1.0, p[:], ALU.mult, ALU.mult, accum_out=neg_sum[:])
-        z_inv2 = sb.tile([P, 1], F32, name="z_inv2")
+        gate = tile("gate", [P, SLOTS], F32, "slot_s")
+        nc.scalar.activation(gate[:], sig_neg[:], ACT.Identity, bias=neg_gain_col[:], scale=gain_col[:])
+        z_inv2 = tile("z_inv2", [P, 1], F32)
         nc.scalar.activation(z_inv2[:], z_inv[:], ACT.Square)
-        centred = sb.tile([P, SLOTS], F32, name="centred")
+        centred = tile("centred", [P, SLOTS], F32)
         nc.scalar.activation(centred[:], c_ps[:], ACT.Identity, bias=neg_sum[:], scale=z[:])
-        weight = sb.tile([P, SLOTS], F32, name="weight")
+        weight = tile("weight", [P, SLOTS], F32)
         nc.vector.scalar_tensor_tensor(weight[:], p[:], z_inv2[:], gate[:], ALU.mult, ALU.mult)
         nc.vector.tensor_tensor(placed[:].indirect(offsets[:]), weight[:], centred[:], ALU.mult)
 
         start = 0
         for n, width in enumerate(OUT_WIDTHS):
             cols = slice(start, start + width)
-            total = sb.tile([P, width], F32, name="total%d" % n)
+            total = tile("total%d" % n, [P, width], F32)
             nc.vector.tensor_tensor(total[:], placed[:, cols], old_sb[:, cols], ALU.add)
             nc.sync.dma_start(out[:, cols], total[:])
             start = start + width

@@ -37,7 +37,7 @@ def tile_attend_bheldback_s_kernel(tc, query, query2, keys_words, keys_scales, s
             return sb.tile(shape, dtype, name=name, tag=slot or name, align_bytes=64)
 
         def load_rows(raw, x):
-            nc.sync.dma_start(raw[:], x.rearrange("(p j) w -> p j w", j=PACK))
+            nc.sync.dma_start(raw, x.rearrange("(p j) w -> p j w", j=PACK))
 
         def load_words(pool_words, words):
             nc.sync.dma_start(pool_words[:].bitcast(I32), words[0].rearrange("p n t -> p (n t)").bitcast(I32))
@@ -57,7 +57,7 @@ def tile_attend_bheldback_s_kernel(tc, query, query2, keys_words, keys_scales, s
         offsets = sb.tile([P, SLOTS // 16], U16, name="offsets")
         nc.sync.dma_start(offsets[:], offs)
         q2_raw = tile("q2_raw", [P, PACK, Q], F32, "slot_vw")
-        load_rows(q2_raw, query2)
+        load_rows(q2_raw[:], query2)
 
         warm_in = tile("warm_in", [P, 1], F32, "slot_q")
         warm_out = tile("warm_out", [P, 1], F32, "slot_vb")
@@ -73,8 +73,11 @@ def tile_attend_bheldback_s_kernel(tc, query, query2, keys_words, keys_scales, s
         nc.vector.tensor_scalar(floor_col[:], one_col[:], LN_FLOOR, None, ALU.mult)
         k_words = tile("k_words", [P, T], U32, "slot_kw")
         load_words(k_words, keys_words)
-        q_raw = tile("q_raw", [P, PACK, Q], F32, "slot_q")
+        q_strict = tile("q_strict", [P, PACK * Q + 8], F32, "slot_q")
+        q_raw = q_strict[:, 0:PACK * Q].rearrange("p (j w) -> p j w", j=PACK)
+        strict_col = q_strict[:, PACK * Q:PACK * Q + 1]
         load_rows(q_raw, query)
+        nc.sync.dma_start(strict_col, strict)
         placed = tile("placed", [P, T], F32)
         nc.vector.memset(placed[:], 0.0)
         v_bytes = tile("v_bytes", [P, T], U8, "slot_vb")
@@ -92,12 +95,10 @@ def tile_attend_bheldback_s_kernel(tc, query, query2, keys_words, keys_scales, s
         q2_scales = tile("q2_scales", [P, Q], U8)
         quantise(q2_codes, q2_scales, q2_bf)
         g_raw = tile("g_raw", [P, PACK, Q], F32, "slot_g")
-        load_rows(g_raw, gout)
+        load_rows(g_raw[:], gout)
 
         q_bf = tile("q_bf", [P, Q, PACK], BF16)
-        nc.scalar.activation(q_bf[:], q_raw[:].rearrange("p j w -> p w j"), ACT.Copy)
-        strict_col = tile("strict_col", [P, 1], F32, "slot_q")
-        nc.sync.dma_start(strict_col[:], strict)
+        nc.scalar.activation(q_bf[:], q_raw.rearrange("p j w -> p w j"), ACT.Copy)
 
         kg_words = tile("kg_words", [P, SLOTS], U32, "slot_kb")
         halves = [slice(h * HALF, (h + 1) * HALF) for h in range(2)]
@@ -129,9 +130,9 @@ def tile_attend_bheldback_s_kernel(tc, query, query2, keys_words, keys_scales, s
         g_bf = tile("g_bf", [P, Q, PACK], BF16)
         nc.gpsimd.tensor_scalar(g_bf[:], g_raw[:].rearrange("p j w -> p w j"), 1.0, 0.0, ALU.mult, ALU.add)
         gain_col = tile("gain_col", [P, 1], F32)
-        nc.gpsimd.tensor_scalar(gain_col[:], strict_col[:], GAIN, 0.0, ALU.mult, ALU.add)
+        nc.gpsimd.tensor_scalar(gain_col[:], strict_col, GAIN, 0.0, ALU.mult, ALU.add)
         neg_gain_col = tile("neg_gain_col", [P, 1], F32)
-        nc.gpsimd.tensor_scalar(neg_gain_col[:], strict_col[:], -GAIN, 0.0, ALU.mult, ALU.add)
+        nc.gpsimd.tensor_scalar(neg_gain_col[:], strict_col, -GAIN, 0.0, ALU.mult, ALU.add)
 
         neg_sp = tile("neg_sp", [P, SLOTS], F32, "slot_vw")
         s = tile("s", [P, SLOTS], F32, "slot_s")
@@ -139,7 +140,7 @@ def tile_attend_bheldback_s_kernel(tc, query, query2, keys_words, keys_scales, s
             nc.vector.scalar_tensor_tensor(neg_sp[:, halves[h]], b_ps[h][:], -1.0, log_sig[:, halves[h]],
                                            ALU.mult, ALU.min)
         for h in range(2):
-            nc.vector.scalar_tensor_tensor(s[:, halves[h]], neg_sp[:, halves[h]], strict_col[:],
+            nc.vector.scalar_tensor_tensor(s[:, halves[h]], neg_sp[:, halves[h]], strict_col,
                                            a_ps[:, halves[h]], ALU.mult, ALU.add)
         g_codes = tile("g_codes", [P, Q], U32)
         g_scales = tile("g_scales", [P, Q], U8)
@@ -172,5 +173,5 @@ def tile_attend_bheldback_s_kernel(tc, query, query2, keys_words, keys_scales, s
             cols = slice(start, start + width)
             total = tile("total%d" % n, [P, width], F32)
             nc.vector.tensor_tensor(total[:], placed[:, cols], old_sb[:, cols], ALU.add)
-            nc.sync.dma_start(out[:, cols], total[:])
+            (nc.sync, nc.scalar)[n % 2].dma_start(out[:, cols], total[:])
             start = start + width

from contextlib import ExitStack

import concourse.mybir as mybir

F32 = mybir.dt.float32
BF16 = mybir.dt.bfloat16
I32 = mybir.dt.int32
U32 = mybir.dt.uint32
U16 = mybir.dt.uint16
U8 = mybir.dt.uint8
FP8X4 = mybir.dt.float8_e4m3fn_x4
ALU = mybir.AluOpType
ACT = mybir.ActivationFunctionType
AXIS_X = mybir.AxisListType.X

P = 128
PACK = 4
T = 2048
SLOTS = 512
HALF = SLOTS // 2
Q = 128
GAIN = 512.0
LN_FLOOR = 2.0 ** -60
OUT_WIDTHS = (256, 512, 512, 512, 256)

FLOPS = 3 * 2 * 512 * Q * SLOTS


def tile_attend_bheldback_s_kernel(tc, query, query2, keys_words, keys_scales, strict, gout,
                                    vals_words, vals_scales, old, offs, out):
    nc = tc.nc
    with ExitStack() as ctx:
        sb = ctx.enter_context(tc.tile_pool(name="sb", bufs=1))
        ps = ctx.enter_context(tc.psum_pool(name="ps", bufs=1))

        def tile(name, shape, dtype, slot=None):
            return sb.tile(shape, dtype, name=name, tag=slot or name, align_bytes=64)

        def load_rows(raw, x):
            nc.sync.dma_start(raw, x.rearrange("(p j) w -> p j w", j=PACK))

        def load_words(pool_words, words):
            nc.sync.dma_start(pool_words[:].bitcast(I32), words[0].rearrange("p n t -> p (n t)").bitcast(I32))

        def load_scale_rows(pool_bytes, scales):
            for r in range(4):
                nc.sync.dma_start(pool_bytes[r:P:32, :].bitcast(I32), scales[0][r:16:4, :].bitcast(I32))

        def quantise(codes, scale_bytes, grouped):
            nc.vector.quantize_mx(out=codes[:].bitcast(FP8X4), scales=scale_bytes[:],
                                  in_=grouped[:].rearrange("p w j -> p (w j)"))

        def product(acc, lhs_codes, lhs_scales, words, scale_bytes):
            nc.tensor.matmul_mx(out=acc, lhsT=lhs_codes.bitcast(FP8X4), lhsT_scale=lhs_scales,
                                rhs=words.bitcast(FP8X4), rhs_scale=scale_bytes, start=True, stop=True)

        offsets = sb.tile([P, SLOTS // 16], U16, name="offsets")
        nc.sync.dma_start(offsets[:], offs)
        q2_raw = tile("q2_raw", [P, PACK, Q], F32, "slot_vw")
        load_rows(q2_raw[:], query2)

        warm_in = tile("warm_in", [P, 1], F32, "slot_q")
        warm_out = tile("warm_out", [P, 1], F32, "slot_vb")
        nc.gpsimd.memset(warm_in[:], 0.0)
        nc.scalar.activation(warm_out[:], warm_in[:], ACT.Sigmoid)

        one_col = tile("one_col", [P, 1], F32, "slot_kw")
        nc.gpsimd.memset(one_col[:], 1.0)
        k_bytes = tile("k_bytes", [P, T], U8, "slot_kb")
        nc.vector.memset(k_bytes[:].bitcast(I32), 0)
        load_scale_rows(k_bytes, keys_scales)
        floor_col = tile("floor_col", [P, 1], F32)
        nc.vector.tensor_scalar(floor_col[:], one_col[:], LN_FLOOR, None, ALU.mult)
        k_words = tile("k_words", [P, T], U32, "slot_kw")
        load_words(k_words, keys_words)
        q_strict = tile("q_strict", [P, PACK * Q + 8], F32, "slot_q")
        q_raw = q_strict[:, 0:PACK * Q].rearrange("p (j w) -> p j w", j=PACK)
        strict_col = q_strict[:, PACK * Q:PACK * Q + 1]
        load_rows(q_raw, query)
        nc.sync.dma_start(strict_col, strict)
        placed = tile("placed", [P, T], F32)
        nc.vector.memset(placed[:], 0.0)
        v_bytes = tile("v_bytes", [P, T], U8, "slot_vb")
        nc.vector.memset(v_bytes[:].bitcast(I32), 0)
        load_scale_rows(v_bytes, vals_scales)

        q2_bf = tile("q2_bf", [P, Q, PACK], BF16, "slot_g")
        nc.scalar.activation(q2_bf[:], q2_raw[:].rearrange("p j w -> p w j"), ACT.Copy)
        v_words = tile("v_words", [P, T], U32, "slot_vw")
        load_words(v_words, vals_words)

        kg_bytes = tile("kg_bytes", [P, SLOTS], U8)
        nc.vector.tensor_copy(kg_bytes[:], k_bytes[:].indirect(offsets[:]))
        q2_codes = tile("q2_codes", [P, Q], U32)
        q2_scales = tile("q2_scales", [P, Q], U8)
        quantise(q2_codes, q2_scales, q2_bf)
        g_raw = tile("g_raw", [P, PACK, Q], F32, "slot_g")
        load_rows(g_raw[:], gout)

        q_bf = tile("q_bf", [P, Q, PACK], BF16)
        nc.scalar.activation(q_bf[:], q_raw.rearrange("p j w -> p w j"), ACT.Copy)

        kg_words = tile("kg_words", [P, SLOTS], U32, "slot_kb")
        halves = [slice(h * HALF, (h + 1) * HALF) for h in range(2)]
        b_ps = [ps.tile([P, HALF], F32, name="b_ps%d" % h) for h in range(2)]
        sig_neg = tile("sig_neg", [P, SLOTS], F32)
        for h in range(2):
            cols = halves[h]
            nc.vector.tensor_copy(kg_words[:, cols],
                                  k_words[:].indirect(offsets[:, h * HALF // 16:(h + 1) * HALF // 16]))
            product(b_ps[h][:], q2_codes[:], q2_scales[:], kg_words[:, cols], kg_bytes[:, cols])
            nc.scalar.activation(sig_neg[:, cols], b_ps[h][:], ACT.Sigmoid, scale=-1.0)
        q_codes = tile("q_codes", [P, Q], U32)
        q_scales = tile("q_scales", [P, Q], U8)
        quantise(q_codes, q_scales, q_bf)
        a_ps = ps.tile([P, SLOTS], F32, name="a_ps")
        product(a_ps[:], q_codes[:], q_scales[:], kg_words[:], kg_bytes[:])

        old_sb = tile("old_sb", [P, T], F32, "slot_kw")
        nc.sync.dma_start(old_sb[:], old)

        log_sig = tile("log_sig", [P, SLOTS], F32)
        for h in range(2):
            nc.scalar.activation(log_sig[:, halves[h]], sig_neg[:, halves[h]], ACT.Ln, bias=floor_col[:])

        vg_bytes = tile("vg_bytes", [P, SLOTS], U8)
        nc.vector.tensor_copy(vg_bytes[:], v_bytes[:].indirect(offsets[:]))
        vg_words = tile("vg_words", [P, SLOTS], U32, "slot_vb")
        nc.vector.tensor_copy(vg_words[:], v_words[:].indirect(offsets[:]))
        g_bf = tile("g_bf", [P, Q, PACK], BF16)
        nc.gpsimd.tensor_scalar(g_bf[:], g_raw[:].rearrange("p j w -> p w j"), 1.0, 0.0, ALU.mult, ALU.add)
        gain_col = tile("gain_col", [P, 1], F32)
        nc.gpsimd.tensor_scalar(gain_col[:], strict_col, GAIN, 0.0, ALU.mult, ALU.add)
        neg_gain_col = tile("neg_gain_col", [P, 1], F32)
        nc.gpsimd.tensor_scalar(neg_gain_col[:], strict_col, -GAIN, 0.0, ALU.mult, ALU.add)

        neg_sp = tile("neg_sp", [P, SLOTS], F32, "slot_vw")
        s = tile("s", [P, SLOTS], F32, "slot_s")
        for h in range(2):
            nc.vector.scalar_tensor_tensor(neg_sp[:, halves[h]], b_ps[h][:], -1.0, log_sig[:, halves[h]],
                                           ALU.mult, ALU.min)
        for h in range(2):
            nc.vector.scalar_tensor_tensor(s[:, halves[h]], neg_sp[:, halves[h]], strict_col,
                                           a_ps[:, halves[h]], ALU.mult, ALU.add)
        g_codes = tile("g_codes", [P, Q], U32)
        g_scales = tile("g_scales", [P, Q], U8)
        quantise(g_codes, g_scales, g_bf)
        c_ps = ps.tile([P, SLOTS], F32, name="c_ps")
        product(c_ps[:], g_codes[:], g_scales[:], vg_words[:], vg_bytes[:])
        neg_max = tile("neg_max", [P, 1], F32)
        nc.vector.tensor_reduce(neg_max[:], s[:], AXIS_X, ALU.max, negate=True)

        p = tile("p", [P, SLOTS], F32)
        z = tile("z", [P, 1], F32)
        nc.scalar.activation(p[:], s[:], ACT.Exp, bias=neg_max[:], accum_out=z[:])
        z_inv = tile("z_inv", [P, 1], F32)
        nc.vector.reciprocal(z_inv[:], z[:])
        neg_cp = tile("neg_cp", [P, SLOTS], F32)
        neg_sum = tile("neg_sum", [P, 1], F32)
        nc.vector.scalar_tensor_tensor(neg_cp[:], c_ps[:], -1.0, p[:], ALU.mult, ALU.mult, accum_out=neg_sum[:])
        gate = tile("gate", [P, SLOTS], F32, "slot_s")
        nc.scalar.activation(gate[:], sig_neg[:], ACT.Identity, bias=neg_gain_col[:], scale=gain_col[:])
        z_inv2 = tile("z_inv2", [P, 1], F32)
        nc.scalar.activation(z_inv2[:], z_inv[:], ACT.Square)
        centred = tile("centred", [P, SLOTS], F32)
        nc.scalar.activation(centred[:], c_ps[:], ACT.Identity, bias=neg_sum[:], scale=z[:])
        weight = tile("weight", [P, SLOTS], F32)
        nc.vector.scalar_tensor_tensor(weight[:], p[:], z_inv2[:], gate[:], ALU.mult, ALU.mult)
        nc.vector.tensor_tensor(placed[:].indirect(offsets[:]), weight[:], centred[:], ALU.mult)

        start = 0
        for n, width in enumerate(OUT_WIDTHS):
            cols = slice(start, start + width)
            total = tile("total%d" % n, [P, width], F32)
            nc.vector.tensor_tensor(total[:], placed[:, cols], old_sb[:, cols], ALU.add)
            (nc.sync, nc.scalar)[n % 2].dma_start(out[:, cols], total[:])
            start = start + width
